import numpy as np
import ml_dtypes


def mxq(x, axis, fmt="e4m3"):
    dtype, down = {"e4m3": (ml_dtypes.float8_e4m3fn, 7), "e5m2": (ml_dtypes.float8_e5m2, 14)}[fmt]
    v = np.moveaxis(np.asarray(x, np.float32).astype(ml_dtypes.bfloat16).astype(np.float64), axis, -1)
    blocks = v.reshape(v.shape[:-1] + (-1, 32))
    amax = np.abs(blocks).max(-1, keepdims=True)
    byte = np.maximum(np.where(amax > 0, np.frexp(amax)[1] - 1 + 127, 0) - down, 1)
    scale = np.exp2(byte - 127.0)
    codes = (blocks / scale).astype(np.float32).astype(dtype).astype(np.float64)
    return np.moveaxis((codes * scale).reshape(v.shape), -1, axis)


WIDE = False


def mx_kscale(k):
    if not WIDE:
        return np.ones(k)
    levels = np.array([30, -30])
    if k % 512:
        return np.exp2(np.random.permutation(np.resize(levels, k // 32))).repeat(32)
    a = np.empty((k // 512, 16))
    for p in range(k // 512):
        a[p, :8] = np.random.permutation(np.resize(levels, 8))
        for g in range(8):
            far = levels[np.abs(levels - a[p, g]) >= 10]
            a[p, g + 8] = far[np.random.randint(len(far))]
    return np.exp2(a.ravel()).repeat(32)


def f64(x):
    return np.asarray(x).astype(np.float64)


def striped(idx):
    return np.tile(np.asarray(idx).reshape(-1, 16).T, (8, 1)).astype(np.uint16)


def unstriped(offs):
    return offs[:16].T.reshape(-1).astype(np.int64)


E2M1 = np.array([0.0, 0.5, 1.0, 1.5, 2.0, 3.0, 4.0, 6.0, -0.0, -0.5, -1.0, -1.5, -2.0, -3.0, -4.0, -6.0])


def pack_weight(w, fmt):
    k, n = w.shape
    w = f64(np.asarray(w, np.float32).astype(ml_dtypes.bfloat16)).reshape(k // 32, 32, n)
    amax = np.abs(w).max(1)
    if fmt in ("e4m3", "e5m2"):
        byte = np.frexp(amax)[1] - 1 + 127 - (7 if fmt == "e4m3" else 14)
    else:
        mant, ex = np.frexp(amax / 6.0)
        byte = np.where(mant > 0.5, ex, ex - 1) + 127
    byte = np.clip(np.where(amax > 0, byte, 1), 1, 254)
    scaled = (w * np.exp2(127.0 - byte)[:, None, :]).reshape(k, n).astype(np.float32)
    by_word = np.ascontiguousarray(scaled.reshape(k // 512, 128, 4, n).transpose(0, 1, 3, 2))
    if fmt in ("e4m3", "e5m2"):
        words = by_word.astype(ml_dtypes.float8_e4m3fn if fmt == "e4m3" else ml_dtypes.float8_e5m2).view(np.uint8)
    else:
        c = by_word.astype(ml_dtypes.float4_e2m1fn).view(np.uint8) & 0xF
        words = (c[..., 0::2] | (c[..., 1::2] << 4)).reshape(k // 512, 128, 2 * n)
    return np.ascontiguousarray(words), np.ascontiguousarray(byte.astype(np.uint8).reshape(k // 512, 16, n))


def unpack_weight(words, scales, fmt):
    g, _, n = scales.shape
    words = np.ascontiguousarray(words).reshape(g, 128, n, -1)
    if fmt in ("e4m3", "e5m2"):
        vals = words.view(ml_dtypes.float8_e4m3fn if fmt == "e4m3" else ml_dtypes.float8_e5m2).astype(np.float64)
    else:
        nib = np.empty((g, 128, n, 4), np.uint8)
        nib[..., 0::2] = words & 0xF
        nib[..., 1::2] = words >> 4
        vals = E2M1[nib]
    vals = vals * np.repeat(np.exp2(scales.astype(np.float64) - 127.0), 8, axis=1)[..., None]
    return vals.transpose(0, 1, 3, 2).reshape(g * 512, n)


def bf(x):
    return np.asarray(x, np.float32).astype(ml_dtypes.bfloat16)


def planes(Y):
    r, m = Y.shape
    b = f64(bf(Y)).reshape(r // 32, 32, m)
    amax = np.abs(b).max(1)
    byte = np.clip(np.where(amax > 0, np.frexp(amax)[1] - 1 + 127 - 7, 1), 1, 254)
    codes = (b * np.exp2(127.0 - byte)[:, None, :]).reshape(r, m).astype(np.float32).astype(ml_dtypes.float8_e4m3fn).view(np.uint8)
    words = codes.reshape(r // 512, 128, 4, m).transpose(0, 1, 3, 2)
    return np.ascontiguousarray(words), np.ascontiguousarray(byte.astype(np.uint8).reshape(r // 512, 16, m))


K, T, J, S, R, V, N, Q = 1024, 1024, 256, 512, 512, 512, 512, 64


def setup_inputs():
    n = np.random.standard_normal
    idx = np.random.permutation(T)[:J]
    idx2 = np.random.permutation(S)[:J]
    idx3 = np.random.permutation(V)[:J]
    idx4 = np.random.permutation(V)[:J]
    fk = mx_kscale(K)
    fr = mx_kscale(R)
    wp = pack_weight(n((K, R)) * 1 / np.sqrt(K) * fk[:, None] * fr, "e2m1")
    wbp = pack_weight(n((R, N)) * 1 / np.sqrt(R) / fr[:, None], "e5m2")
    return {
        "xa": (n((K, T))).astype(np.float32),
        "xb": (n((K, S))).astype(np.float32),
        "fk": (np.random.uniform(0.5, 2.0, (K, 1)) / fk[:, None]).astype(np.float32),
        "w_words": wp[0],
        "w_scales": wp[1],
        "tb": (n((R, V)) * 0.7 * fr[:, None]).astype(np.float32),
        "wb_words": wbp[0],
        "wb_scales": wbp[1],
        "rw": (np.random.uniform(0.5, 2.0, (1, J))).astype(np.float32),
        "qw": (np.random.uniform(0.5, 2.0, (1, Q))).astype(np.float32),
        "offs": striped(idx),
        "offs2": striped(idx2),
        "offs3": striped(idx3),
        "offs4": striped(idx4),
    }


def reference(xa, xb, fk, w_words, w_scales, tb, wb_words, wb_scales, rw, qw, offs, offs2, offs3, offs4):
    idx = unstriped(offs)
    idx2 = unstriped(offs2)
    idx3 = unstriped(offs3)
    idx4 = unstriped(offs4)
    wu = unpack_weight(w_words, w_scales, "e2m1")
    wbu = unpack_weight(wb_words, wb_scales, "e5m2")
    u = f64(xa)[:, idx] * f64(xb)[:, idx2] * f64(fk)
    uq = mxq(u, 0, "e4m3")
    a = wu.T @ uq
    hid = np.maximum(a + f64(tb)[:, idx3] - f64(tb)[:, idx4], 0.0)
    hidq = mxq(hid, 0, "e5m2")
    p = wbu.T @ hidq
    y = (p * f64(rw)).reshape(N, Q, J // Q).sum(axis=2) * f64(qw)
    words, scales = planes(y)
    return y, words, scales

@@ -1,0 +1,221 @@
+from contextlib import ExitStack
+
+import concourse.mybir as mybir
+from concourse.masks import make_identity
+
+K, T, J, S, R, V, N, Q = 1024, 1024, 256, 512, 512, 512, 512, 64
+FLOPS = 2 * K * R * J + 2 * R * N * J
+
+F32 = mybir.dt.float32
+BF16 = mybir.dt.bfloat16
+I32 = mybir.dt.int32
+U32 = mybir.dt.uint32
+U16 = mybir.dt.uint16
+U8 = mybir.dt.uint8
+E4M3 = mybir.dt.float8_e4m3fn_x4
+E5M2 = mybir.dt.float8_e5m2_x4
+E2M1 = mybir.dt.float4_e2m1fn_x4
+ALU = mybir.AluOpType
+ACT = mybir.ActivationFunctionType
+AXIS = mybir.AxisListType
+
+P = 128
+PACK = 4
+PASSES = K // (P * PACK)
+HALVES = 2
+JH = J // HALVES
+SET = J // Q
+QH = Q // HALVES
+
+
+def tile_list_entryproducts_tworeach_groupsums_pl_kernel(
+    tc, xa, xb, fk, w_words, w_scales, tb, wb_words, wb_scales, rw, qw, offs, offs2, offs3, offs4, out_0, out_1, out_2
+):
+    nc = tc.nc
+    with ExitStack() as ctx:
+        lists = ctx.enter_context(tc.tile_pool(name="lists", bufs=1))
+        sb = ctx.enter_context(tc.tile_pool(name="sb", bufs=1))
+        ps = ctx.enter_context(tc.psum_pool(name="ps", bufs=1))
+
+        def load_list(src, name):
+            tile = lists.tile([P, J // 16], U16, name=name)
+            nc.sync.dma_start(tile[:], src)
+            return tile
+
+        def load_planes(src, row0, t0, count, name):
+            width = src.shape[1]
+            tile = sb.tile([P, count, width], F32, name=name)
+            rows = src[row0 : row0 + P * PACK, :].rearrange("(p t) c -> p t c", t=PACK)
+            nc.sync.dma_start(tile[:], rows[:, t0 : t0 + count, :])
+            return [tile[:, e, :] for e in range(count)]
+
+        def gather(on_scalar, out, window, offsets):
+            if on_scalar:
+                nc.scalar.activation(out, window.indirect(offsets[:]), ACT.Copy)
+            else:
+                nc.vector.tensor_copy(out, window.indirect(offsets[:]))
+
+        ws_raw = sb.tile([P, PASSES, R], U8, name="ws_raw")
+        wbs_raw = sb.tile([P, N], U8, name="wbs_raw")
+        nc.vector.memset(ws_raw[:].bitcast(I32), 0)
+        nc.vector.memset(wbs_raw[:].bitcast(I32), 0)
+        fk_sb = sb.tile([P, PASSES, PACK], F32, name="fk_sb")
+        nc.scalar.dma_start(fk_sb[:], fk.rearrange("(a p t) o -> p a (t o)", p=P, t=PACK))
+        rw_sb = sb.tile([P, SET], F32, name="rw_sb")
+        qw_sb = sb.tile([P, 1], F32, name="qw_sb")
+        nc.vector.memset(rw_sb[Q:P, :], 0.0)
+        nc.vector.memset(qw_sb[Q:P, :], 0.0)
+        nc.scalar.dma_start(rw_sb[0:Q, :], rw.rearrange("o (q i) -> (o q) i", i=SET))
+        nc.scalar.dma_start(qw_sb[0:Q, :], qw.rearrange("o (q i) -> (o q) i", i=1))
+
+        ident = sb.tile([P, P], F32, name="ident")
+        make_identity(nc, ident[:])
+
+        w_raw = sb.tile([P, PASSES, 2 * R], U8, name="w_raw")
+        nc.sync.dma_start(w_raw[:].bitcast(I32), w_words.rearrange("a p c -> p a c").bitcast(I32))
+        list_a = load_list(offs, "list_a")
+        xa_planes = [load_planes(xa, 0, 0, 2, "xa_00")]
+        list_b = load_list(offs2, "list_b")
+        xb_planes = [load_planes(xb, 0, 0, 4, "xb_0")]
+        for quad in range(4):
+            nc.sync.dma_start(
+                ws_raw[32 * quad : 32 * quad + 4, :, :].bitcast(I32),
+                w_scales[:, 4 * quad : 4 * quad + 4, :].rearrange("a r c -> r a c").bitcast(I32),
+            )
+        xa_planes[0].extend(load_planes(xa, 0, 2, 2, "xa_01"))
+        list_plus = load_list(offs3, "list_plus")
+        list_minus = load_list(offs4, "list_minus")
+        tb_planes = load_planes(tb, 0, 0, 4, "tb_sb")
+        for quad in range(4):
+            nc.sync.dma_start(
+                wbs_raw[32 * quad : 32 * quad + 4, :].bitcast(I32),
+                wb_scales[0, 4 * quad : 4 * quad + 4, :].bitcast(I32),
+            )
+        xa_planes.append(load_planes(xa, 512, 0, 2, "xa_10"))
+        xa_planes[1].extend(load_planes(xa, 512, 2, 2, "xa_11"))
+        xb_planes.append(load_planes(xb, 512, 0, 2, "xb_10"))
+        xb_planes[1].extend(load_planes(xb, 512, 2, 2, "xb_11"))
+        wb_raw = sb.tile([P, N], U32, name="wb_raw")
+        nc.sync.dma_start(wb_raw[:].bitcast(I32), wb_words[0].rearrange("p c r -> p (c r)").bitcast(I32))
+
+        w_dealt = sb.tile([P, PASSES, PACK, 2 * P], U8, name="w_dealt", align_bytes=64)
+        nc.vector.tensor_copy(
+            w_dealt[:].bitcast(U16),
+            w_raw[:].bitcast(U16).rearrange("p a (m t) -> p a t m", t=PACK),
+        )
+
+        cw_col = sb.tile([P, SET], F32, name="cw_col")
+        nc.vector.tensor_scalar(cw_col[:], rw_sb[:], qw_sb[:], None, ALU.mult)
+        cw_ps = ps.tile([P, SET, P], F32, name="cw_ps")
+        for i in range(SET):
+            nc.tensor.transpose(cw_ps[:, i, :], cw_col[:, i : i + 1].to_broadcast([P, P]), ident[:])
+        cw = sb.tile([P, Q, SET], F32, name="cw")
+        nc.scalar.copy(cw[:], cw_ps[:, :, 0:Q].rearrange("p i q -> p q i"))
+
+        acc_a = [ps.tile([P, PACK, JH], F32, name="acc_a%d" % h) for h in range(HALVES)]
+        ws_dealt = sb.tile([P, PASSES, PACK, P], U8, name="ws_dealt", align_bytes=64)
+        wbs_dealt = sb.tile([P, PACK, P], U8, name="wbs_dealt", align_bytes=64)
+
+        def first_stage(a):
+            ga = sb.tile([P, PACK, J], F32, name="ga%d" % a)
+            gs = sb.tile([P, PACK, J], F32, name="gs%d" % a)
+            gb = sb.tile([P, PACK, J], F32, name="gb%d" % a)
+            for t in range(PACK):
+                gather(t % 2 == 0, ga[:, t, :], xa_planes[a][t], list_a)
+                nc.scalar.activation(gs[:, t, :], ga[:, t, :], ACT.Copy, scale=fk_sb[:, a, t : t + 1])
+            for t in range(PACK):
+                gather(t % 2 == 0, gb[:, t, :], xb_planes[a][t], list_b)
+            u_bf = [sb.tile([P, JH * PACK], BF16, name="u_bf%d%d" % (a, h), align_bytes=64) for h in range(HALVES)]
+            for h in range(HALVES):
+                cols = slice(h * JH, (h + 1) * JH)
+                nc.vector.tensor_tensor(
+                    u_bf[h][:].rearrange("p (c i t) -> p c t i", i=4, t=PACK),
+                    gs[:, :, cols].rearrange("p t (c i) -> p c t i", i=4),
+                    gb[:, :, cols].rearrange("p t (c i) -> p c t i", i=4),
+                    ALU.mult,
+                )
+            for h in range(HALVES):
+                codes = sb.tile([P, JH], U32, name="u_codes%d%d" % (a, h), align_bytes=64)
+                scales = sb.tile([P, JH], U8, name="u_scales%d%d" % (a, h), align_bytes=64)
+                nc.vector.quantize_mx(codes[:].bitcast(E4M3), scales[:], u_bf[h][:])
+                for t in range(PACK):
+                    nc.tensor.matmul_mx(
+                        acc_a[h][:, t, :],
+                        lhsT=w_dealt[:, a, t, :].bitcast(E2M1),
+                        lhsT_scale=ws_dealt[:, a, t, :],
+                        rhs=codes[:].bitcast(E4M3),
+                        rhs_scale=scales[:],
+                        start=(a == 0 and t == 0),
+                        stop=(a == PASSES - 1 and t == PACK - 1),
+                    )
+
+        nc.vector.tensor_copy(ws_dealt[:], ws_raw[:].rearrange("p a (m t) -> p a t m", t=PACK))
+        first_stage(0)
+
+        g_plus = sb.tile([P, PACK, J], F32, name="g_plus")
+        g_minus = sb.tile([P, PACK, J], F32, name="g_minus")
+        for t in range(PACK):
+            gather(True, g_minus[:, t, :], tb_planes[t], list_minus)
+            gather(t % 2 == 1, g_plus[:, t, :], tb_planes[t], list_plus)
+        nc.vector.tensor_copy(wbs_dealt[:], wbs_raw[:].rearrange("p (m t) -> p t m", t=PACK))
+        diff = sb.tile([P, PACK, J], F32, name="diff")
+        nc.vector.tensor_tensor(diff[:], g_plus[:], g_minus[:], ALU.subtract)
+
+        first_stage(1)
+
+        wb_dealt = sb.tile([P, PACK, P], U32, name="wb_dealt", align_bytes=64)
+        nc.vector.tensor_copy(wb_dealt[:], wb_raw[:].rearrange("p (m t) -> p t m", t=PACK))
+
+        pre = [sb.tile([P, PACK, JH], F32, name="pre%d" % h) for h in range(HALVES)]
+        hid_bf = [sb.tile([P, JH * PACK], BF16, name="hid_bf%d" % h, align_bytes=64) for h in range(HALVES)]
+        for h in range(HALVES):
+            nc.vector.tensor_tensor(pre[h][:], acc_a[h][:], diff[:, :, h * JH : (h + 1) * JH], ALU.add)
+        woven = [hid_bf[h][:].rearrange("p (c i t) -> p c t i", i=4, t=PACK) for h in range(HALVES)]
+        plain = [pre[h][:].rearrange("p t (c i) -> p c t i", i=4) for h in range(HALVES)]
+        nc.scalar.activation(woven[0], plain[0], ACT.Relu)
+        nc.vector.tensor_scalar(woven[1], plain[1], 0.0, None, ALU.max)
+
+        acc_p = [ps.tile([P, PACK, JH], F32, name="acc_p%d" % h) for h in range(HALVES)]
+        for h in range(HALVES):
+            codes = sb.tile([P, JH], U32, name="h_codes%d" % h, align_bytes=64)
+            scales = sb.tile([P, JH], U8, name="h_scales%d" % h, align_bytes=64)
+            nc.vector.quantize_mx(codes[:].bitcast(E5M2), scales[:], hid_bf[h][:])
+            for t in range(PACK):
+                nc.tensor.matmul_mx(
+                    acc_p[h][:, t, :],
+                    lhsT=wb_dealt[:, t, :].bitcast(E5M2),
+                    lhsT_scale=wbs_dealt[:, t, :],
+                    rhs=codes[:].bitcast(E5M2),
+                    rhs_scale=scales[:],
+                    start=True,
+                    stop=True,
+                )
+
+        weighted = [sb.tile([P, PACK, JH], F32, name="weighted%d" % h) for h in range(HALVES)]
+        y = sb.tile([P, PACK, Q], F32, name="y")
+        for h in range(HALVES):
+            cw_half = cw[:, h * QH : (h + 1) * QH, :].rearrange("p q i -> p (q i)")
+            nc.vector.tensor_tensor(
+                weighted[h][:], acc_p[h][:], cw_half.unsqueeze(1).to_broadcast([P, PACK, JH]), ALU.mult
+            )
+        for h in range(HALVES):
+            nc.vector.tensor_reduce(
+                y[:, :, h * QH : (h + 1) * QH],
+                weighted[h][:].rearrange("p t (q i) -> p t q i", i=SET),
+                AXIS.X,
+                ALU.add,
+            )
+        nc.sync.dma_start(out_0.rearrange("(p t) q -> p t q", t=PACK), y[:])
+
+        y_bf = sb.tile([P, Q * PACK], BF16, name="y_bf", align_bytes=64)
+        nc.vector.tensor_copy(y_bf[:].rearrange("p (q t) -> p q t", t=PACK), y[:].rearrange("p t q -> p q t"))
+        y_codes = sb.tile([P, Q], U32, name="y_codes", align_bytes=64)
+        y_scales = sb.tile([P, Q], U8, name="y_scales", align_bytes=64)
+        nc.vector.quantize_mx(y_codes[:].bitcast(E4M3), y_scales[:], y_bf[:])
+        nc.sync.dma_start(out_1[0].rearrange("p c r -> p (c r)").bitcast(I32), y_codes[:].bitcast(I32))
+        for quad in range(4):
+            queue = nc.scalar if quad % 2 == 0 else nc.sync
+            queue.dma_start(
+                out_2[0, 4 * quad : 4 * quad + 4, :].bitcast(I32),
+                y_scales[32 * quad : 32 * quad + 4, :].bitcast(I32),
+            )

@@ -17,7 +17,6 @@ E5M2 = mybir.dt.float8_e5m2_x4
 E2M1 = mybir.dt.float4_e2m1fn_x4
 ALU = mybir.AluOpType
 ACT = mybir.ActivationFunctionType
-AXIS = mybir.AxisListType
 
 P = 128
 PACK = 4
@@ -51,9 +50,9 @@ def tile_list_entryproducts_tworeach_groupsums_pl_kernel(
 
         def gather(on_scalar, out, window, offsets):
             if on_scalar:
-                nc.scalar.activation(out, window.indirect(offsets[:]), ACT.Copy)
+                nc.scalar.activation(out, window.indirect(offsets), ACT.Copy)
             else:
-                nc.vector.tensor_copy(out, window.indirect(offsets[:]))
+                nc.vector.tensor_copy(out, window.indirect(offsets))
 
         ws_raw = sb.tile([P, PASSES, R], U8, name="ws_raw")
         wbs_raw = sb.tile([P, N], U8, name="wbs_raw")
@@ -71,10 +70,14 @@ def tile_list_entryproducts_tworeach_groupsums_pl_kernel(
         ident = sb.tile([P, P], F32, name="ident")
         make_identity(nc, ident[:])
 
+        tb_planes = load_planes(tb, 0, 0, 2, "tb_0")
+        list_plus = load_list(offs3, "list_plus")
+        list_minus = load_list(offs4, "list_minus")
+        tb_planes.extend(load_planes(tb, 0, 2, 1, "tb_2"))
+        xa_planes = [load_planes(xa, 0, 0, 2, "xa_00")]
+        list_a = load_list(offs, "list_a")
         w_raw = sb.tile([P, PASSES, 2 * R], U8, name="w_raw")
         nc.sync.dma_start(w_raw[:].bitcast(I32), w_words.rearrange("a p c -> p a c").bitcast(I32))
-        list_a = load_list(offs, "list_a")
-        xa_planes = [load_planes(xa, 0, 0, 2, "xa_00")]
         list_b = load_list(offs2, "list_b")
         xb_planes = [load_planes(xb, 0, 0, 4, "xb_0")]
         for quad in range(4):
@@ -83,25 +86,32 @@ def tile_list_entryproducts_tworeach_groupsums_pl_kernel(
                 w_scales[:, 4 * quad : 4 * quad + 4, :].rearrange("a r c -> r a c").bitcast(I32),
             )
         xa_planes[0].extend(load_planes(xa, 0, 2, 2, "xa_01"))
-        list_plus = load_list(offs3, "list_plus")
-        list_minus = load_list(offs4, "list_minus")
-        tb_planes = load_planes(tb, 0, 0, 4, "tb_sb")
+        xa_planes.append(load_planes(xa, 512, 0, 2, "xa_10"))
         for quad in range(4):
             nc.sync.dma_start(
                 wbs_raw[32 * quad : 32 * quad + 4, :].bitcast(I32),
                 wb_scales[0, 4 * quad : 4 * quad + 4, :].bitcast(I32),
             )
-        xa_planes.append(load_planes(xa, 512, 0, 2, "xa_10"))
         xa_planes[1].extend(load_planes(xa, 512, 2, 2, "xa_11"))
         xb_planes.append(load_planes(xb, 512, 0, 2, "xb_10"))
-        xb_planes[1].extend(load_planes(xb, 512, 2, 2, "xb_11"))
+        xb_planes[1].extend(load_planes(xb, 512, 2, 1, "xb_12"))
+        xb_planes[1].extend(load_planes(xb, 512, 3, 1, "xb_13"))
+        tb_planes.extend(load_planes(tb, 0, 3, 1, "tb_3"))
         wb_raw = sb.tile([P, N], U32, name="wb_raw")
         nc.sync.dma_start(wb_raw[:].bitcast(I32), wb_words[0].rearrange("p c r -> p (c r)").bitcast(I32))
 
+        g_plus = sb.tile([P, PACK, J], F32, name="g_plus")
+        g_minus = sb.tile([P, PACK, J], F32, name="g_minus")
+        for t in range(PACK - 1):
+            gather(True, g_minus[:, t, :], tb_planes[t], list_minus[:])
+            gather(False, g_plus[:, t, :], tb_planes[t], list_plus[:])
+        diff = sb.tile([P, PACK, J], F32, name="diff")
+        nc.vector.tensor_tensor(diff[:, 0:3, :], g_plus[:, 0:3, :], g_minus[:, 0:3, :], ALU.subtract)
+
         w_dealt = sb.tile([P, PASSES, PACK, 2 * P], U8, name="w_dealt", align_bytes=64)
         nc.vector.tensor_copy(
-            w_dealt[:].bitcast(U16),
-            w_raw[:].bitcast(U16).rearrange("p a (m t) -> p a t m", t=PACK),
+            w_dealt[:].bitcast(U16).rearrange("p a t (c i) -> p a c t i", i=8),
+            w_raw[:].bitcast(U16).rearrange("p a (c i t) -> p a c t i", i=8, t=PACK),
         )
 
         cw_col = sb.tile([P, SET], F32, name="cw_col")
@@ -119,19 +129,20 @@ def tile_list_entryproducts_tworeach_groupsums_pl_kernel(
         def first_stage(a):
             ga = sb.tile([P, PACK, J], F32, name="ga%d" % a)
             gs = sb.tile([P, PACK, J], F32, name="gs%d" % a)
-            gb = sb.tile([P, PACK, J], F32, name="gb%d" % a)
+            gb = [sb.tile([P, PACK, JH], F32, name="gb%d%d" % (a, h)) for h in range(HALVES)]
             for t in range(PACK):
-                gather(t % 2 == 0, ga[:, t, :], xa_planes[a][t], list_a)
+                gather(t % 2 == 0, ga[:, t, :], xa_planes[a][t], list_a[:])
                 nc.scalar.activation(gs[:, t, :], ga[:, t, :], ACT.Copy, scale=fk_sb[:, a, t : t + 1])
             for t in range(PACK):
-                gather(t % 2 == 0, gb[:, t, :], xb_planes[a][t], list_b)
+                for h in range(HALVES):
+                    gather(h == 0, gb[h][:, t, :], xb_planes[a][t], list_b[:, h * JH // 16 : (h + 1) * JH // 16])
             u_bf = [sb.tile([P, JH * PACK], BF16, name="u_bf%d%d" % (a, h), align_bytes=64) for h in range(HALVES)]
             for h in range(HALVES):
                 cols = slice(h * JH, (h + 1) * JH)
                 nc.vector.tensor_tensor(
                     u_bf[h][:].rearrange("p (c i t) -> p c t i", i=4, t=PACK),
                     gs[:, :, cols].rearrange("p t (c i) -> p c t i", i=4),
-                    gb[:, :, cols].rearrange("p t (c i) -> p c t i", i=4),
+                    gb[h][:].rearrange("p t (c i) -> p c t i", i=4),
                     ALU.mult,
                 )
             for h in range(HALVES):
@@ -149,22 +160,27 @@ def tile_list_entryproducts_tworeach_groupsums_pl_kernel(
                         stop=(a == PASSES - 1 and t == PACK - 1),
                     )
 
-        nc.vector.tensor_copy(ws_dealt[:], ws_raw[:].rearrange("p a (m t) -> p a t m", t=PACK))
+        nc.vector.tensor_copy(
+            ws_dealt[:].rearrange("p a t (c i) -> p a c t i", i=16),
+            ws_raw[:].rearrange("p a (c i t) -> p a c t i", i=16, t=PACK),
+        )
         first_stage(0)
 
-        g_plus = sb.tile([P, PACK, J], F32, name="g_plus")
-        g_minus = sb.tile([P, PACK, J], F32, name="g_minus")
-        for t in range(PACK):
-            gather(True, g_minus[:, t, :], tb_planes[t], list_minus)
-            gather(t % 2 == 1, g_plus[:, t, :], tb_planes[t], list_plus)
-        nc.vector.tensor_copy(wbs_dealt[:], wbs_raw[:].rearrange("p (m t) -> p t m", t=PACK))
-        diff = sb.tile([P, PACK, J], F32, name="diff")
-        nc.vector.tensor_tensor(diff[:], g_plus[:], g_minus[:], ALU.subtract)
+        nc.vector.tensor_copy(
+            wbs_dealt[:].rearrange("p t (c i) -> p c t i", i=16),
+            wbs_raw[:].rearrange("p (c i t) -> p c t i", i=16, t=PACK),
+        )
 
         first_stage(1)
 
         wb_dealt = sb.tile([P, PACK, P], U32, name="wb_dealt", align_bytes=64)
-        nc.vector.tensor_copy(wb_dealt[:], wb_raw[:].rearrange("p (m t) -> p t m", t=PACK))
+        gather(True, g_minus[:, 3, :], tb_planes[3], list_minus[:])
+        gather(True, g_plus[:, 3, :], tb_planes[3], list_plus[:])
+        nc.vector.tensor_copy(
+            wb_dealt[:].rearrange("p t (c i) -> p c t i", i=4),
+            wb_raw[:].rearrange("p (c i t) -> p c t i", i=4, t=PACK),
+        )
+        nc.vector.tensor_tensor(diff[:, 3, :], g_plus[:, 3, :], g_minus[:, 3, :], ALU.subtract)
 
         pre = [sb.tile([P, PACK, JH], F32, name="pre%d" % h) for h in range(HALVES)]
         hid_bf = [sb.tile([P, JH * PACK], BF16, name="hid_bf%d" % h, align_bytes=64) for h in range(HALVES)]
@@ -172,8 +188,8 @@ def tile_list_entryproducts_tworeach_groupsums_pl_kernel(
             nc.vector.tensor_tensor(pre[h][:], acc_a[h][:], diff[:, :, h * JH : (h + 1) * JH], ALU.add)
         woven = [hid_bf[h][:].rearrange("p (c i t) -> p c t i", i=4, t=PACK) for h in range(HALVES)]
         plain = [pre[h][:].rearrange("p t (c i) -> p c t i", i=4) for h in range(HALVES)]
-        nc.scalar.activation(woven[0], plain[0], ACT.Relu)
-        nc.vector.tensor_scalar(woven[1], plain[1], 0.0, None, ALU.max)
+        for h in range(HALVES):
+            nc.scalar.activation(woven[h], plain[h], ACT.Relu)
 
         acc_p = [ps.tile([P, PACK, JH], F32, name="acc_p%d" % h) for h in range(HALVES)]
         for h in range(HALVES):
@@ -198,17 +214,20 @@ def tile_list_entryproducts_tworeach_groupsums_pl_kernel(
             nc.vector.tensor_tensor(
                 weighted[h][:], acc_p[h][:], cw_half.unsqueeze(1).to_broadcast([P, PACK, JH]), ALU.mult
             )
+        pairs = sb.tile([P, PACK, Q, 2], F32, name="pairs")
         for h in range(HALVES):
-            nc.vector.tensor_reduce(
-                y[:, :, h * QH : (h + 1) * QH],
-                weighted[h][:].rearrange("p t (q i) -> p t q i", i=SET),
-                AXIS.X,
-                ALU.add,
-            )
+            by_set = weighted[h][:].rearrange("p t (q i) -> p t q i", i=SET)
+            nc.vector.tensor_tensor(pairs[:, :, h * QH : (h + 1) * QH, :], by_set[:, :, :, 0:2], by_set[:, :, :, 2:4], ALU.add)
+        y_bf = sb.tile([P, Q * PACK], BF16, name="y_bf", align_bytes=64)
+        nc.vector.tensor_tensor(
+            y_bf[:].rearrange("p (c e t) -> p c t e", e=2, t=PACK),
+            pairs[:, :, :, 0].rearrange("p t (c e) -> p c t e", e=2),
+            pairs[:, :, :, 1].rearrange("p t (c e) -> p c t e", e=2),
+            ALU.add,
+        )
+        nc.vector.tensor_tensor(y[:], pairs[:, :, :, 0], pairs[:, :, :, 1], ALU.add)
         nc.sync.dma_start(out_0.rearrange("(p t) q -> p t q", t=PACK), y[:])
 
-        y_bf = sb.tile([P, Q * PACK], BF16, name="y_bf", align_bytes=64)
-        nc.vector.tensor_copy(y_bf[:].rearrange("p (q t) -> p q t", t=PACK), y[:].rearrange("p t q -> p q t"))
         y_codes = sb.tile([P, Q], U32, name="y_codes", align_bytes=64)
         y_scales = sb.tile([P, Q], U8, name="y_scales", align_bytes=64)
         nc.vector.quantize_mx(y_codes[:].bitcast(E4M3), y_scales[:], y_bf[:])

@@ -70,14 +70,11 @@ def tile_list_entryproducts_tworeach_groupsums_pl_kernel(
         ident = sb.tile([P, P], F32, name="ident")
         make_identity(nc, ident[:])
 
-        tb_planes = load_planes(tb, 0, 0, 2, "tb_0")
+        tb_planes = load_planes(tb, 0, 0, 3, "tb_0")
         list_plus = load_list(offs3, "list_plus")
         list_minus = load_list(offs4, "list_minus")
-        tb_planes.extend(load_planes(tb, 0, 2, 1, "tb_2"))
         xa_planes = [load_planes(xa, 0, 0, 2, "xa_00")]
         list_a = load_list(offs, "list_a")
-        w_raw = sb.tile([P, PASSES, 2 * R], U8, name="w_raw")
-        nc.sync.dma_start(w_raw[:].bitcast(I32), w_words.rearrange("a p c -> p a c").bitcast(I32))
         list_b = load_list(offs2, "list_b")
         xb_planes = [load_planes(xb, 0, 0, 4, "xb_0")]
         for quad in range(4):
@@ -93,6 +90,8 @@ def tile_list_entryproducts_tworeach_groupsums_pl_kernel(
                 wb_scales[0, 4 * quad : 4 * quad + 4, :].bitcast(I32),
             )
         xa_planes[1].extend(load_planes(xa, 512, 2, 2, "xa_11"))
+        w_raw = sb.tile([P, PASSES, 2 * R], U8, name="w_raw")
+        nc.sync.dma_start(w_raw[:].bitcast(I32), w_words.rearrange("a p c -> p a c").bitcast(I32))
         xb_planes.append(load_planes(xb, 512, 0, 2, "xb_10"))
         xb_planes[1].extend(load_planes(xb, 512, 2, 1, "xb_12"))
         xb_planes[1].extend(load_planes(xb, 512, 3, 1, "xb_13"))
@@ -108,12 +107,6 @@ def tile_list_entryproducts_tworeach_groupsums_pl_kernel(
         diff = sb.tile([P, PACK, J], F32, name="diff")
         nc.vector.tensor_tensor(diff[:, 0:3, :], g_plus[:, 0:3, :], g_minus[:, 0:3, :], ALU.subtract)
 
-        w_dealt = sb.tile([P, PASSES, PACK, 2 * P], U8, name="w_dealt", align_bytes=64)
-        nc.vector.tensor_copy(
-            w_dealt[:].bitcast(U16).rearrange("p a t (c i) -> p a c t i", i=8),
-            w_raw[:].bitcast(U16).rearrange("p a (c i t) -> p a c t i", i=8, t=PACK),
-        )
-
         cw_col = sb.tile([P, SET], F32, name="cw_col")
         nc.vector.tensor_scalar(cw_col[:], rw_sb[:], qw_sb[:], None, ALU.mult)
         cw_ps = ps.tile([P, SET, P], F32, name="cw_ps")
@@ -126,52 +119,69 @@ def tile_list_entryproducts_tworeach_groupsums_pl_kernel(
         ws_dealt = sb.tile([P, PASSES, PACK, P], U8, name="ws_dealt", align_bytes=64)
         wbs_dealt = sb.tile([P, PACK, P], U8, name="wbs_dealt", align_bytes=64)
 
-        def first_stage(a):
+        w_dealt = sb.tile([P, PASSES, PACK, 2 * P], U8, name="w_dealt", align_bytes=64)
+        gs = [sb.tile([P, PACK, J], F32, name="gs%d" % a) for a in range(PASSES)]
+        gb = [[sb.tile([P, PACK, JH], F32, name="gb%d%d" % (a, h)) for h in range(HALVES)] for a in range(PASSES)]
+        u_codes = [[sb.tile([P, JH], U32, name="u_codes%d%d" % (a, h), align_bytes=64) for h in range(HALVES)] for a in range(PASSES)]
+        u_scales = [[sb.tile([P, JH], U8, name="u_scales%d%d" % (a, h), align_bytes=64) for h in range(HALVES)] for a in range(PASSES)]
+
+        def pick_xa(a):
             ga = sb.tile([P, PACK, J], F32, name="ga%d" % a)
-            gs = sb.tile([P, PACK, J], F32, name="gs%d" % a)
-            gb = [sb.tile([P, PACK, JH], F32, name="gb%d%d" % (a, h)) for h in range(HALVES)]
             for t in range(PACK):
                 gather(t % 2 == 0, ga[:, t, :], xa_planes[a][t], list_a[:])
-                nc.scalar.activation(gs[:, t, :], ga[:, t, :], ACT.Copy, scale=fk_sb[:, a, t : t + 1])
-            for t in range(PACK):
+                nc.scalar.activation(gs[a][:, t, :], ga[:, t, :], ACT.Copy, scale=fk_sb[:, a, t : t + 1])
+
+        def pick_xb(a, planes):
+            for t in planes:
                 for h in range(HALVES):
-                    gather(h == 0, gb[h][:, t, :], xb_planes[a][t], list_b[:, h * JH // 16 : (h + 1) * JH // 16])
+                    gather(h == 1, gb[a][h][:, t, :], xb_planes[a][t], list_b[:, h * JH // 16 : (h + 1) * JH // 16])
+
+        def quantise_u(a):
             u_bf = [sb.tile([P, JH * PACK], BF16, name="u_bf%d%d" % (a, h), align_bytes=64) for h in range(HALVES)]
             for h in range(HALVES):
                 cols = slice(h * JH, (h + 1) * JH)
                 nc.vector.tensor_tensor(
                     u_bf[h][:].rearrange("p (c i t) -> p c t i", i=4, t=PACK),
-                    gs[:, :, cols].rearrange("p t (c i) -> p c t i", i=4),
-                    gb[h][:].rearrange("p t (c i) -> p c t i", i=4),
+                    gs[a][:, :, cols].rearrange("p t (c i) -> p c t i", i=4),
+                    gb[a][h][:].rearrange("p t (c i) -> p c t i", i=4),
                     ALU.mult,
                 )
             for h in range(HALVES):
-                codes = sb.tile([P, JH], U32, name="u_codes%d%d" % (a, h), align_bytes=64)
-                scales = sb.tile([P, JH], U8, name="u_scales%d%d" % (a, h), align_bytes=64)
-                nc.vector.quantize_mx(codes[:].bitcast(E4M3), scales[:], u_bf[h][:])
+                nc.vector.quantize_mx(u_codes[a][h][:].bitcast(E4M3), u_scales[a][h][:], u_bf[h][:])
+
+        def first_product(a):
+            for h in range(HALVES):
                 for t in range(PACK):
                     nc.tensor.matmul_mx(
                         acc_a[h][:, t, :],
                         lhsT=w_dealt[:, a, t, :].bitcast(E2M1),
                         lhsT_scale=ws_dealt[:, a, t, :],
-                        rhs=codes[:].bitcast(E4M3),
-                        rhs_scale=scales[:],
+                        rhs=u_codes[a][h][:].bitcast(E4M3),
+                        rhs_scale=u_scales[a][h][:],
                         start=(a == 0 and t == 0),
                         stop=(a == PASSES - 1 and t == PACK - 1),
                     )
 
+        pick_xa(0)
+        pick_xb(0, range(PACK))
+        quantise_u(0)
         nc.vector.tensor_copy(
             ws_dealt[:].rearrange("p a t (c i) -> p a c t i", i=16),
             ws_raw[:].rearrange("p a (c i t) -> p a c t i", i=16, t=PACK),
         )
-        first_stage(0)
-
         nc.vector.tensor_copy(
             wbs_dealt[:].rearrange("p t (c i) -> p c t i", i=16),
             wbs_raw[:].rearrange("p (c i t) -> p c t i", i=16, t=PACK),
         )
-
-        first_stage(1)
+        pick_xa(1)
+        nc.vector.tensor_copy(
+            w_dealt[:].bitcast(U16).rearrange("p a t (c i) -> p a c t i", i=8),
+            w_raw[:].bitcast(U16).rearrange("p a (c i t) -> p a c t i", i=8, t=PACK),
+        )
+        first_product(0)
+        pick_xb(1, range(PACK))
+        quantise_u(1)
+        first_product(1)
 
         wb_dealt = sb.tile([P, PACK, P], U32, name="wb_dealt", align_bytes=64)
         gather(True, g_minus[:, 3, :], tb_planes[3], list_minus[:])
@@ -191,14 +201,14 @@ def tile_list_entryproducts_tworeach_groupsums_pl_kernel(
         for h in range(HALVES):
             nc.scalar.activation(woven[h], plain[h], ACT.Relu)
 
-        acc_p = [ps.tile([P, PACK, JH], F32, name="acc_p%d" % h) for h in range(HALVES)]
+        acc_p = [[ps.tile([P, 2, JH], F32, name="acc_p%d%d" % (h, u)) for u in range(2)] for h in range(HALVES)]
         for h in range(HALVES):
             codes = sb.tile([P, JH], U32, name="h_codes%d" % h, align_bytes=64)
             scales = sb.tile([P, JH], U8, name="h_scales%d" % h, align_bytes=64)
             nc.vector.quantize_mx(codes[:].bitcast(E5M2), scales[:], hid_bf[h][:])
             for t in range(PACK):
                 nc.tensor.matmul_mx(
-                    acc_p[h][:, t, :],
+                    acc_p[h][t // 2][:, t % 2, :],
                     lhsT=wb_dealt[:, t, :].bitcast(E5M2),
                     lhsT_scale=wbs_dealt[:, t, :],
                     rhs=codes[:].bitcast(E5M2),
@@ -207,25 +217,44 @@ def tile_list_entryproducts_tworeach_groupsums_pl_kernel(
                     stop=True,
                 )
 
-        weighted = [sb.tile([P, PACK, JH], F32, name="weighted%d" % h) for h in range(HALVES)]
         y = sb.tile([P, PACK, Q], F32, name="y")
-        for h in range(HALVES):
-            cw_half = cw[:, h * QH : (h + 1) * QH, :].rearrange("p q i -> p (q i)")
-            nc.vector.tensor_tensor(
-                weighted[h][:], acc_p[h][:], cw_half.unsqueeze(1).to_broadcast([P, PACK, JH]), ALU.mult
-            )
         pairs = sb.tile([P, PACK, Q, 2], F32, name="pairs")
-        for h in range(HALVES):
-            by_set = weighted[h][:].rearrange("p t (q i) -> p t q i", i=SET)
-            nc.vector.tensor_tensor(pairs[:, :, h * QH : (h + 1) * QH, :], by_set[:, :, :, 0:2], by_set[:, :, :, 2:4], ALU.add)
+        parts = [(h, u) for h in range(HALVES) for u in range(2)]
+        weighted = [sb.tile([P, 2, JH], F32, name="weighted%d%d" % part) for part in parts]
+
+        def weigh(n):
+            h, u = parts[n]
+            cw_half = cw[:, h * QH : (h + 1) * QH, :].rearrange("p q i -> p (q i)")
+            nc.vector.tensor_tensor(weighted[n][:], acc_p[h][u][:], cw_half.unsqueeze(1).to_broadcast([P, 2, JH]), ALU.mult)
+
         y_bf = sb.tile([P, Q * PACK], BF16, name="y_bf", align_bytes=64)
-        nc.vector.tensor_tensor(
-            y_bf[:].rearrange("p (c e t) -> p c t e", e=2, t=PACK),
-            pairs[:, :, :, 0].rearrange("p t (c e) -> p c t e", e=2),
-            pairs[:, :, :, 1].rearrange("p t (c e) -> p c t e", e=2),
-            ALU.add,
-        )
-        nc.vector.tensor_tensor(y[:], pairs[:, :, :, 0], pairs[:, :, :, 1], ALU.add)
+        y_woven = y_bf[:].rearrange("p (q t) -> p t q", t=PACK)
+
+        def add_pairs(engine, n):
+            h, u = parts[n]
+            by_set = weighted[n][:].rearrange("p t (q i) -> p t q i", i=SET)
+            engine.tensor_tensor(
+                pairs[:, 2 * u : 2 * u + 2, h * QH : (h + 1) * QH, :], by_set[:, :, :, 0:2], by_set[:, :, :, 2:4], ALU.add
+            )
+
+        def finish(out, h):
+            cols = slice(h * QH, (h + 1) * QH)
+            nc.vector.tensor_tensor(
+                out[:, :, cols].rearrange("p t (c e) -> p c t e", e=2),
+                pairs[:, :, cols, 0].rearrange("p t (c e) -> p c t e", e=2),
+                pairs[:, :, cols, 1].rearrange("p t (c e) -> p c t e", e=2),
+                ALU.add,
+            )
+
+        for n in range(3):
+            weigh(n)
+            add_pairs(nc.gpsimd, n)
+        weigh(3)
+        finish(y_woven, 0)
+        add_pairs(nc.vector, 3)
+        finish(y[:], 0)
+        finish(y_woven, 1)
+        finish(y[:], 1)
         nc.sync.dma_start(out_0.rearrange("(p t) q -> p t q", t=PACK), y[:])
 
         y_codes = sb.tile([P, Q], U32, name="y_codes", align_bytes=64)

@@ -104,8 +104,10 @@ def tile_list_entryproducts_tworeach_groupsums_pl_kernel(
         for t in range(PACK - 1):
             gather(True, g_minus[:, t, :], tb_planes[t], list_minus[:])
             gather(False, g_plus[:, t, :], tb_planes[t], list_plus[:])
-        diff = sb.tile([P, PACK, J], F32, name="diff")
-        nc.vector.tensor_tensor(diff[:, 0:3, :], g_plus[:, 0:3, :], g_minus[:, 0:3, :], ALU.subtract)
+        diff = [sb.tile([P, PACK, JH], F32, name="diff%d" % h) for h in range(HALVES)]
+        for h in range(HALVES):
+            cols = slice(h * JH, (h + 1) * JH)
+            nc.vector.tensor_tensor(diff[h][:, 0:3, :], g_plus[:, 0:3, cols], g_minus[:, 0:3, cols], ALU.subtract)
 
         cw_col = sb.tile([P, SET], F32, name="cw_col")
         nc.vector.tensor_scalar(cw_col[:], rw_sb[:], qw_sb[:], None, ALU.mult)
@@ -184,18 +186,22 @@ def tile_list_entryproducts_tworeach_groupsums_pl_kernel(
         first_product(1)
 
         wb_dealt = sb.tile([P, PACK, P], U32, name="wb_dealt", align_bytes=64)
-        gather(True, g_minus[:, 3, :], tb_planes[3], list_minus[:])
-        gather(True, g_plus[:, 3, :], tb_planes[3], list_plus[:])
+        for h in range(HALVES):
+            cols = slice(h * JH, (h + 1) * JH)
+            gather(True, g_minus[:, 3, cols], tb_planes[3], list_minus[:, h * JH // 16 : (h + 1) * JH // 16])
+            gather(True, g_plus[:, 3, cols], tb_planes[3], list_plus[:, h * JH // 16 : (h + 1) * JH // 16])
         nc.vector.tensor_copy(
             wb_dealt[:].rearrange("p t (c i) -> p c t i", i=4),
             wb_raw[:].rearrange("p (c i t) -> p c t i", i=4, t=PACK),
         )
-        nc.vector.tensor_tensor(diff[:, 3, :], g_plus[:, 3, :], g_minus[:, 3, :], ALU.subtract)
+        for h in range(HALVES):
+            cols = slice(h * JH, (h + 1) * JH)
+            nc.vector.tensor_tensor(diff[h][:, 3, :], g_plus[:, 3, cols], g_minus[:, 3, cols], ALU.subtract)
 
         pre = [sb.tile([P, PACK, JH], F32, name="pre%d" % h) for h in range(HALVES)]
         hid_bf = [sb.tile([P, JH * PACK], BF16, name="hid_bf%d" % h, align_bytes=64) for h in range(HALVES)]
         for h in range(HALVES):
-            nc.vector.tensor_tensor(pre[h][:], acc_a[h][:], diff[:, :, h * JH : (h + 1) * JH], ALU.add)
+            nc.vector.tensor_tensor(pre[h][:], acc_a[h][:], diff[h][:], ALU.add)
         woven = [hid_bf[h][:].rearrange("p (c i t) -> p c t i", i=4, t=PACK) for h in range(HALVES)]
         plain = [pre[h][:].rearrange("p t (c i) -> p c t i", i=4) for h in range(HALVES)]
         for h in range(HALVES):
@@ -237,10 +243,14 @@ def tile_list_entryproducts_tworeach_groupsums_pl_kernel(
                 pairs[:, 2 * u : 2 * u + 2, h * QH : (h + 1) * QH, :], by_set[:, :, :, 0:2], by_set[:, :, :, 2:4], ALU.add
             )
 
-        def finish(out, h):
+        def finish_plain(h):
+            cols = slice(h * QH, (h + 1) * QH)
+            nc.vector.tensor_tensor(y[:, :, cols], pairs[:, :, cols, 0], pairs[:, :, cols, 1], ALU.add)
+
+        def finish_woven(h):
             cols = slice(h * QH, (h + 1) * QH)
             nc.vector.tensor_tensor(
-                out[:, :, cols].rearrange("p t (c e) -> p c t e", e=2),
+                y_woven[:, :, cols].rearrange("p t (c e) -> p c t e", e=2),
                 pairs[:, :, cols, 0].rearrange("p t (c e) -> p c t e", e=2),
                 pairs[:, :, cols, 1].rearrange("p t (c e) -> p c t e", e=2),
                 ALU.add,
@@ -250,11 +260,11 @@ def tile_list_entryproducts_tworeach_groupsums_pl_kernel(
             weigh(n)
             add_pairs(nc.gpsimd, n)
         weigh(3)
-        finish(y_woven, 0)
+        finish_woven(0)
         add_pairs(nc.vector, 3)
-        finish(y[:], 0)
-        finish(y_woven, 1)
-        finish(y[:], 1)
+        finish_plain(0)
+        finish_woven(1)
+        finish_plain(1)
         nc.sync.dma_start(out_0.rearrange("(p t) q -> p t q", t=PACK), y[:])
 
         y_codes = sb.tile([P, Q], U32, name="y_codes", align_bytes=64)

from contextlib import ExitStack

import concourse.mybir as mybir
from concourse.masks import make_identity

K, T, J, S, R, V, N, Q = 1024, 1024, 256, 512, 512, 512, 512, 64
FLOPS = 2 * K * R * J + 2 * R * N * J

F32 = mybir.dt.float32
BF16 = mybir.dt.bfloat16
I32 = mybir.dt.int32
U32 = mybir.dt.uint32
U16 = mybir.dt.uint16
U8 = mybir.dt.uint8
E4M3 = mybir.dt.float8_e4m3fn_x4
E5M2 = mybir.dt.float8_e5m2_x4
E2M1 = mybir.dt.float4_e2m1fn_x4
ALU = mybir.AluOpType
ACT = mybir.ActivationFunctionType

P = 128
PACK = 4
PASSES = K // (P * PACK)
HALVES = 2
JH = J // HALVES
SET = J // Q
QH = Q // HALVES


def tile_list_entryproducts_tworeach_groupsums_pl_kernel(
    tc, xa, xb, fk, w_words, w_scales, tb, wb_words, wb_scales, rw, qw, offs, offs2, offs3, offs4, out_0, out_1, out_2
):
    nc = tc.nc
    with ExitStack() as ctx:
        lists = ctx.enter_context(tc.tile_pool(name="lists", bufs=1))
        sb = ctx.enter_context(tc.tile_pool(name="sb", bufs=1))
        ps = ctx.enter_context(tc.psum_pool(name="ps", bufs=1))

        def load_list(src, name):
            tile = lists.tile([P, J // 16], U16, name=name)
            nc.sync.dma_start(tile[:], src)
            return tile

        def load_planes(src, row0, t0, count, name):
            width = src.shape[1]
            tile = sb.tile([P, count, width], F32, name=name)
            rows = src[row0 : row0 + P * PACK, :].rearrange("(p t) c -> p t c", t=PACK)
            nc.sync.dma_start(tile[:], rows[:, t0 : t0 + count, :])
            return [tile[:, e, :] for e in range(count)]

        def gather(on_scalar, out, window, offsets):
            if on_scalar:
                nc.scalar.activation(out, window.indirect(offsets), ACT.Copy)
            else:
                nc.vector.tensor_copy(out, window.indirect(offsets))

        ws_raw = sb.tile([P, PASSES, R], U8, name="ws_raw")
        wbs_raw = sb.tile([P, N], U8, name="wbs_raw")
        nc.vector.memset(ws_raw[:].bitcast(I32), 0)
        nc.vector.memset(wbs_raw[:].bitcast(I32), 0)
        fk_sb = sb.tile([P, PASSES, PACK], F32, name="fk_sb")
        nc.scalar.dma_start(fk_sb[:], fk.rearrange("(a p t) o -> p a (t o)", p=P, t=PACK))
        rw_sb = sb.tile([P, SET], F32, name="rw_sb")
        qw_sb = sb.tile([P, 1], F32, name="qw_sb")
        nc.vector.memset(rw_sb[Q:P, :], 0.0)
        nc.vector.memset(qw_sb[Q:P, :], 0.0)
        nc.scalar.dma_start(rw_sb[0:Q, :], rw.rearrange("o (q i) -> (o q) i", i=SET))
        nc.scalar.dma_start(qw_sb[0:Q, :], qw.rearrange("o (q i) -> (o q) i", i=1))

        ident = sb.tile([P, P], F32, name="ident")
        make_identity(nc, ident[:])

        tb_planes = load_planes(tb, 0, 0, 3, "tb_0")
        list_plus = load_list(offs3, "list_plus")
        list_minus = load_list(offs4, "list_minus")
        xa_planes = [load_planes(xa, 0, 0, 2, "xa_00")]
        list_a = load_list(offs, "list_a")
        list_b = load_list(offs2, "list_b")
        xb_planes = [load_planes(xb, 0, 0, 4, "xb_0")]
        for quad in range(4):
            nc.sync.dma_start(
                ws_raw[32 * quad : 32 * quad + 4, :, :].bitcast(I32),
                w_scales[:, 4 * quad : 4 * quad + 4, :].rearrange("a r c -> r a c").bitcast(I32),
            )
        xa_planes[0].extend(load_planes(xa, 0, 2, 2, "xa_01"))
        xa_planes.append(load_planes(xa, 512, 0, 2, "xa_10"))
        for quad in range(4):
            nc.sync.dma_start(
                wbs_raw[32 * quad : 32 * quad + 4, :].bitcast(I32),
                wb_scales[0, 4 * quad : 4 * quad + 4, :].bitcast(I32),
            )
        xa_planes[1].extend(load_planes(xa, 512, 2, 2, "xa_11"))
        w_raw = sb.tile([P, PASSES, 2 * R], U8, name="w_raw")
        nc.sync.dma_start(w_raw[:].bitcast(I32), w_words.rearrange("a p c -> p a c").bitcast(I32))
        xb_planes.append(load_planes(xb, 512, 0, 2, "xb_10"))
        xb_planes[1].extend(load_planes(xb, 512, 2, 1, "xb_12"))
        xb_planes[1].extend(load_planes(xb, 512, 3, 1, "xb_13"))
        tb_planes.extend(load_planes(tb, 0, 3, 1, "tb_3"))
        wb_raw = sb.tile([P, N], U32, name="wb_raw")
        nc.sync.dma_start(wb_raw[:].bitcast(I32), wb_words[0].rearrange("p c r -> p (c r)").bitcast(I32))

        g_plus = sb.tile([P, PACK, J], F32, name="g_plus")
        g_minus = sb.tile([P, PACK, J], F32, name="g_minus")
        for t in range(PACK - 1):
            gather(True, g_minus[:, t, :], tb_planes[t], list_minus[:])
            gather(False, g_plus[:, t, :], tb_planes[t], list_plus[:])
        diff = [sb.tile([P, PACK, JH], F32, name="diff%d" % h) for h in range(HALVES)]
        for h in range(HALVES):
            cols = slice(h * JH, (h + 1) * JH)
            nc.vector.tensor_tensor(diff[h][:, 0:3, :], g_plus[:, 0:3, cols], g_minus[:, 0:3, cols], ALU.subtract)

        cw_col = sb.tile([P, SET], F32, name="cw_col")
        nc.vector.tensor_scalar(cw_col[:], rw_sb[:], qw_sb[:], None, ALU.mult)
        cw_ps = ps.tile([P, SET, P], F32, name="cw_ps")
        for i in range(SET):
            nc.tensor.transpose(cw_ps[:, i, :], cw_col[:, i : i + 1].to_broadcast([P, P]), ident[:])
        cw = sb.tile([P, Q, SET], F32, name="cw")
        nc.scalar.copy(cw[:], cw_ps[:, :, 0:Q].rearrange("p i q -> p q i"))

        acc_a = [ps.tile([P, PACK, JH], F32, name="acc_a%d" % h) for h in range(HALVES)]
        ws_dealt = sb.tile([P, PASSES, PACK, P], U8, name="ws_dealt", align_bytes=64)
        wbs_dealt = sb.tile([P, PACK, P], U8, name="wbs_dealt", align_bytes=64)

        w_dealt = sb.tile([P, PASSES, PACK, 2 * P], U8, name="w_dealt", align_bytes=64)
        gs = [sb.tile([P, PACK, J], F32, name="gs%d" % a) for a in range(PASSES)]
        gb = [[sb.tile([P, PACK, JH], F32, name="gb%d%d" % (a, h)) for h in range(HALVES)] for a in range(PASSES)]
        u_codes = [[sb.tile([P, JH], U32, name="u_codes%d%d" % (a, h), align_bytes=64) for h in range(HALVES)] for a in range(PASSES)]
        u_scales = [[sb.tile([P, JH], U8, name="u_scales%d%d" % (a, h), align_bytes=64) for h in range(HALVES)] for a in range(PASSES)]

        def pick_xa(a):
            ga = sb.tile([P, PACK, J], F32, name="ga%d" % a)
            for t in range(PACK):
                gather(t % 2 == 0, ga[:, t, :], xa_planes[a][t], list_a[:])
                nc.scalar.activation(gs[a][:, t, :], ga[:, t, :], ACT.Copy, scale=fk_sb[:, a, t : t + 1])

        def pick_xb(a, planes):
            for t in planes:
                for h in range(HALVES):
                    gather(h == 1, gb[a][h][:, t, :], xb_planes[a][t], list_b[:, h * JH // 16 : (h + 1) * JH // 16])

        def quantise_u(a):
            u_bf = [sb.tile([P, JH * PACK], BF16, name="u_bf%d%d" % (a, h), align_bytes=64) for h in range(HALVES)]
            for h in range(HALVES):
                cols = slice(h * JH, (h + 1) * JH)
                nc.vector.tensor_tensor(
                    u_bf[h][:].rearrange("p (c i t) -> p c t i", i=4, t=PACK),
                    gs[a][:, :, cols].rearrange("p t (c i) -> p c t i", i=4),
                    gb[a][h][:].rearrange("p t (c i) -> p c t i", i=4),
                    ALU.mult,
                )
            for h in range(HALVES):
                nc.vector.quantize_mx(u_codes[a][h][:].bitcast(E4M3), u_scales[a][h][:], u_bf[h][:])

        def first_product(a):
            for h in range(HALVES):
                for t in range(PACK):
                    nc.tensor.matmul_mx(
                        acc_a[h][:, t, :],
                        lhsT=w_dealt[:, a, t, :].bitcast(E2M1),
                        lhsT_scale=ws_dealt[:, a, t, :],
                        rhs=u_codes[a][h][:].bitcast(E4M3),
                        rhs_scale=u_scales[a][h][:],
                        start=(a == 0 and t == 0),
                        stop=(a == PASSES - 1 and t == PACK - 1),
                    )

        pick_xa(0)
        pick_xb(0, range(PACK))
        quantise_u(0)
        nc.vector.tensor_copy(
            ws_dealt[:].rearrange("p a t (c i) -> p a c t i", i=16),
            ws_raw[:].rearrange("p a (c i t) -> p a c t i", i=16, t=PACK),
        )
        nc.vector.tensor_copy(
            wbs_dealt[:].rearrange("p t (c i) -> p c t i", i=16),
            wbs_raw[:].rearrange("p (c i t) -> p c t i", i=16, t=PACK),
        )
        pick_xa(1)
        nc.vector.tensor_copy(
            w_dealt[:].bitcast(U16).rearrange("p a t (c i) -> p a c t i", i=8),
            w_raw[:].bitcast(U16).rearrange("p a (c i t) -> p a c t i", i=8, t=PACK),
        )
        first_product(0)
        pick_xb(1, range(PACK))
        quantise_u(1)
        first_product(1)

        wb_dealt = sb.tile([P, PACK, P], U32, name="wb_dealt", align_bytes=64)
        for h in range(HALVES):
            cols = slice(h * JH, (h + 1) * JH)
            gather(True, g_minus[:, 3, cols], tb_planes[3], list_minus[:, h * JH // 16 : (h + 1) * JH // 16])
            gather(True, g_plus[:, 3, cols], tb_planes[3], list_plus[:, h * JH // 16 : (h + 1) * JH // 16])
        nc.vector.tensor_copy(
            wb_dealt[:].rearrange("p t (c i) -> p c t i", i=4),
            wb_raw[:].rearrange("p (c i t) -> p c t i", i=4, t=PACK),
        )
        for h in range(HALVES):
            cols = slice(h * JH, (h + 1) * JH)
            nc.vector.tensor_tensor(diff[h][:, 3, :], g_plus[:, 3, cols], g_minus[:, 3, cols], ALU.subtract)

        pre = [sb.tile([P, PACK, JH], F32, name="pre%d" % h) for h in range(HALVES)]
        hid_bf = [sb.tile([P, JH * PACK], BF16, name="hid_bf%d" % h, align_bytes=64) for h in range(HALVES)]
        for h in range(HALVES):
            nc.vector.tensor_tensor(pre[h][:], acc_a[h][:], diff[h][:], ALU.add)
        woven = [hid_bf[h][:].rearrange("p (c i t) -> p c t i", i=4, t=PACK) for h in range(HALVES)]
        plain = [pre[h][:].rearrange("p t (c i) -> p c t i", i=4) for h in range(HALVES)]
        for h in range(HALVES):
            nc.scalar.activation(woven[h], plain[h], ACT.Relu)

        acc_p = [[ps.tile([P, 2, JH], F32, name="acc_p%d%d" % (h, u)) for u in range(2)] for h in range(HALVES)]
        for h in range(HALVES):
            codes = sb.tile([P, JH], U32, name="h_codes%d" % h, align_bytes=64)
            scales = sb.tile([P, JH], U8, name="h_scales%d" % h, align_bytes=64)
            nc.vector.quantize_mx(codes[:].bitcast(E5M2), scales[:], hid_bf[h][:])
            for t in range(PACK):
                nc.tensor.matmul_mx(
                    acc_p[h][t // 2][:, t % 2, :],
                    lhsT=wb_dealt[:, t, :].bitcast(E5M2),
                    lhsT_scale=wbs_dealt[:, t, :],
                    rhs=codes[:].bitcast(E5M2),
                    rhs_scale=scales[:],
                    start=True,
                    stop=True,
                )

        y = sb.tile([P, PACK, Q], F32, name="y")
        pairs = sb.tile([P, PACK, Q, 2], F32, name="pairs")
        parts = [(h, u) for h in range(HALVES) for u in range(2)]
        weighted = [sb.tile([P, 2, JH], F32, name="weighted%d%d" % part) for part in parts]

        def weigh(n):
            h, u = parts[n]
            cw_half = cw[:, h * QH : (h + 1) * QH, :].rearrange("p q i -> p (q i)")
            nc.vector.tensor_tensor(weighted[n][:], acc_p[h][u][:], cw_half.unsqueeze(1).to_broadcast([P, 2, JH]), ALU.mult)

        y_bf = sb.tile([P, Q * PACK], BF16, name="y_bf", align_bytes=64)
        y_woven = y_bf[:].rearrange("p (q t) -> p t q", t=PACK)

        def add_pairs(engine, n):
            h, u = parts[n]
            by_set = weighted[n][:].rearrange("p t (q i) -> p t q i", i=SET)
            engine.tensor_tensor(
                pairs[:, 2 * u : 2 * u + 2, h * QH : (h + 1) * QH, :], by_set[:, :, :, 0:2], by_set[:, :, :, 2:4], ALU.add
            )

        def finish_plain(h):
            cols = slice(h * QH, (h + 1) * QH)
            nc.vector.tensor_tensor(y[:, :, cols], pairs[:, :, cols, 0], pairs[:, :, cols, 1], ALU.add)

        def finish_woven(h):
            cols = slice(h * QH, (h + 1) * QH)
            nc.vector.tensor_tensor(
                y_woven[:, :, cols].rearrange("p t (c e) -> p c t e", e=2),
                pairs[:, :, cols, 0].rearrange("p t (c e) -> p c t e", e=2),
                pairs[:, :, cols, 1].rearrange("p t (c e) -> p c t e", e=2),
                ALU.add,
            )

        for n in range(3):
            weigh(n)
            add_pairs(nc.gpsimd, n)
        weigh(3)
        finish_woven(0)
        add_pairs(nc.vector, 3)
        finish_plain(0)
        finish_woven(1)
        finish_plain(1)
        nc.sync.dma_start(out_0.rearrange("(p t) q -> p t q", t=PACK), y[:])

        y_codes = sb.tile([P, Q], U32, name="y_codes", align_bytes=64)
        y_scales = sb.tile([P, Q], U8, name="y_scales", align_bytes=64)
        nc.vector.quantize_mx(y_codes[:].bitcast(E4M3), y_scales[:], y_bf[:])
        nc.sync.dma_start(out_1[0].rearrange("p c r -> p (c r)").bitcast(I32), y_codes[:].bitcast(I32))
        for quad in range(4):
            queue = nc.scalar if quad % 2 == 0 else nc.sync
            queue.dma_start(
                out_2[0, 4 * quad : 4 * quad + 4, :].bitcast(I32),
                y_scales[32 * quad : 32 * quad + 4, :].bitcast(I32),
            )
